import numpy as np
import ml_dtypes


def mxq(x, axis, fmt="e4m3"):
    dtype, down = {"e4m3": (ml_dtypes.float8_e4m3fn, 7), "e5m2": (ml_dtypes.float8_e5m2, 14)}[fmt]
    v = np.moveaxis(np.asarray(x, np.float32).astype(ml_dtypes.bfloat16).astype(np.float64), axis, -1)
    blocks = v.reshape(v.shape[:-1] + (-1, 32))
    amax = np.abs(blocks).max(-1, keepdims=True)
    byte = np.maximum(np.where(amax > 0, np.frexp(amax)[1] - 1 + 127, 0) - down, 1)
    scale = np.exp2(byte - 127.0)
    codes = (blocks / scale).astype(np.float32).astype(dtype).astype(np.float64)
    return np.moveaxis((codes * scale).reshape(v.shape), -1, axis)


WIDE = False


def mx_kscale(k):
    if not WIDE:
        return np.ones(k)
    levels = np.array([10, -10, 5, -5, 0])
    if k % 512:
        return np.exp2(np.random.permutation(np.resize(levels, k // 32))).repeat(32)
    a = np.empty((k // 512, 16))
    for p in range(k // 512):
        a[p, :8] = np.random.permutation(np.resize(levels, 8))
        for g in range(8):
            far = levels[np.abs(levels - a[p, g]) >= 10]
            a[p, g + 8] = far[np.random.randint(len(far))]
    return np.exp2(a.ravel()).repeat(32)


def f64(x):
    return np.asarray(x).astype(np.float64)


def striped(idx):
    return np.tile(idx.reshape(-1, 16).T, (8, 1)).astype(np.uint16)


def unstriped(offs):
    return offs[:16].T.reshape(-1).astype(np.int64)


def relu(v):
    return np.maximum(v, 0.0)


K, T, E, C, H, N = 1024, 1536, 2, 256, 1024, 128


def by_expert(wq, xq):
    return np.concatenate([wq[e].T @ xq[:, e * C:(e + 1) * C] for e in range(E)], axis=1)


def setup_inputs():
    n = np.random.standard_normal
    s = mx_kscale(K)[:, None]
    u = mx_kscale(H)
    return {
        "xT": (n((K, T)) * s).astype(np.float32),
        "w1": (n((E, K, H)) / np.sqrt(K) / s[None]).astype(np.float32),
        "w3": (n((E, K, H)) / np.sqrt(K) / s[None] * u[None, None, :]).astype(np.float32),
        "w2": (n((E, H, N)) / np.sqrt(H) / u[None, :, None]).astype(np.float32),
        "gate": np.tile(np.random.uniform(0.2, 1.0, E * C), (N, 1)).astype(np.float32),
        "offs": striped(np.random.permutation(T)[:E * C]),
    }


def reference(xT, w1, w3, w2, gate, offs):
    idx = unstriped(offs)
    xq = mxq(f64(xT)[:, idx], 0, "e4m3")
    h = relu(by_expert(mxq(f64(w1), 1, "e4m3"), xq))
    h = h * by_expert(mxq(f64(w3), 1, "e4m3"), xq)
    y = by_expert(mxq(f64(w2), 1, "e4m3"), mxq(h, 0, "e4m3"))
    out = np.zeros((N, T))
    out[:, idx] = f64(gate) * y
    return out

@@ -1,0 +1,260 @@
+from contextlib import ExitStack
+
+import concourse.mybir as mybir
+
+K, T, E, C, H, N = 1024, 1536, 2, 256, 1024, 128
+FLOPS = 2 * E * C * (2 * K * H + H * N)
+
+F32 = mybir.dt.float32
+BF16 = mybir.dt.bfloat16
+U32 = mybir.dt.uint32
+U16 = mybir.dt.uint16
+U8 = mybir.dt.uint8
+FP8X4 = mybir.dt.float8_e4m3fn_x4
+MULT = mybir.AluOpType.mult
+RELU = mybir.ActivationFunctionType.Relu
+
+P = 128
+PACK = 4
+PASS = P * PACK
+SLOTS = E * C
+HALF = 128
+SHARES = [32] * 4 + [56] * 10 + [72, 88]
+
+
+def tile_routed_moe_kernel(tc, xT, w1, w3, w2, gate, offs, out):
+    nc = tc.nc
+    with ExitStack() as ctx:
+        keep = ctx.enter_context(tc.tile_pool(name="keep", bufs=1))
+        planes = ctx.enter_context(tc.tile_pool(name="planes", bufs=8))
+        raws = ctx.enter_context(tc.tile_pool(name="raws", bufs=8))
+        mids = ctx.enter_context(tc.tile_pool(name="mids", bufs=3))
+        codes = ctx.enter_context(tc.tile_pool(name="codes", bufs=16))
+        toks = ctx.enter_context(tc.tile_pool(name="toks", bufs=2))
+        hid = ctx.enter_context(tc.tile_pool(name="hid", bufs=4))
+        psum = ctx.enter_context(tc.psum_pool(name="psum", bufs=3))
+        psum_y = ctx.enter_context(tc.psum_pool(name="psum_y", bufs=2))
+
+        offsets = keep.tile([P, SLOTS // 16], U16, name="offsets")
+        nc.sync.dma_start(offsets[:], offs)
+        window = keep.tile([P, T], F32, name="window")
+        nc.vector.memset(window[:], 0.0)
+
+        xTv = xT.rearrange("(g p t) n -> g p t n", p=P, t=PACK)
+
+        def load_w(w, e, k, g):
+            raw = raws.tile([P, PACK, PASS], F32, name="raw")
+            src = w[e, k * PASS:(k + 1) * PASS, g * PASS:(g + 1) * PASS]
+            nc.sync.dma_start(raw[:], src.rearrange("(p j) c -> p j c", j=PACK))
+            return raw
+
+        def load_plane(g, t):
+            plane = planes.tile([P, T], F32, name="plane")
+            nc.sync.dma_start(plane[:], xTv[g, :, t, :])
+            return plane
+
+        def load_w2(e):
+            raw = keep.tile([P, 2, PACK, N], F32, name="w2raw%d" % e)
+            nc.sync.dma_start(raw[:], w2[e].rearrange("(g p j) n -> p g j n", p=P, j=PACK))
+            return raw
+
+        def interleave_w(raw, share):
+            mid = mids.tile([P, PACK * PASS], BF16, name="mid", align_bytes=64)
+            dst = mid[:].rearrange("p (t m j) -> p m j t", t=PACK, j=PACK)
+            src = raw[:].rearrange("p j (m t) -> p m j t", t=PACK)
+            if share:
+                nc.vector.tensor_copy(dst[:, 0:share], src[:, 0:share])
+            nc.scalar.copy(dst[:, share:P], src[:, share:P])
+            return mid
+
+        def quantize_w(mid):
+            words = codes.tile([P, PASS], U32, name="words", align_bytes=64)
+            scales = codes.tile([P, PASS], U8, name="scales", align_bytes=64)
+            nc.vector.quantize_mx(out=words[:].bitcast(FP8X4), scales=scales[:], in_=mid[:])
+            return words, scales
+
+        def interleave_x(g4):
+            xi = toks.tile([P, SLOTS, PACK], BF16, name="xi", align_bytes=64)
+            nc.scalar.copy(xi[:].rearrange("p (c i) t -> p c t i", i=4), g4[:].rearrange("p t (c i) -> p c t i", i=4))
+            return xi
+
+        def quantize_x(xi):
+            words = toks.tile([P, SLOTS], U32, name="xwords", align_bytes=64)
+            scales = toks.tile([P, SLOTS], U8, name="xscales", align_bytes=64)
+            nc.vector.quantize_mx(out=words[:].bitcast(FP8X4), scales=scales[:], in_=xi[:].rearrange("p n t -> p (n t)"))
+            return words, scales
+
+        def interleave_w2(e, raw):
+            mid = keep.tile([P, 2, N, PACK], BF16, name="w2mid%d" % e, align_bytes=64)
+            for g, copy in ((0, nc.vector.tensor_copy), (1, nc.scalar.copy)):
+                copy(mid[:, g].rearrange("p (c i) j -> p c j i", i=4), raw[:, g].rearrange("p j (c i) -> p c j i", i=4))
+            return mid
+
+        def quantize_w2(e, mid):
+            words = keep.tile([P, 2 * N], U32, name="w2words%d" % e, align_bytes=64)
+            scales = keep.tile([P, 2 * N], U8, name="w2scales%d" % e, align_bytes=64)
+            nc.vector.quantize_mx(out=words[:].bitcast(FP8X4), scales=scales[:], in_=mid[:].rearrange("p g n j -> p (g n j)"))
+            return words, scales
+
+        xq = []
+        wq = {}
+
+        def matmuls(mat, e, g, s):
+            bank = psum.tile([P, PACK, HALF], F32, name="bank" + mat)
+            cols = slice(e * C + s * HALF, e * C + (s + 1) * HALF)
+            for t in range(PACK):
+                for k in range(2):
+                    words, scales = wq[mat, e, k, g]
+                    nc.tensor.matmul_mx(
+                        out=bank[:, t, :],
+                        lhsT=words[:, t * P:(t + 1) * P].bitcast(FP8X4), lhsT_scale=scales[:, t * P:(t + 1) * P],
+                        rhs=xq[k][0][:, cols].bitcast(FP8X4), rhs_scale=xq[k][1][:, cols],
+                        start=(k == 0), stop=(k == 1))
+            return bank
+
+        def relu(bank):
+            ra = hid.tile([P, HALF, PACK], F32, name="ra")
+            nc.scalar.activation(ra[:], bank[:].rearrange("p t n -> p n t"), RELU)
+            return ra
+
+        def product(bank, ra):
+            h = hid.tile([P, HALF, PACK], BF16, name="h", align_bytes=64)
+            nc.vector.tensor_tensor(h[:], bank[:].rearrange("p t n -> p n t"), ra[:], MULT)
+            return h
+
+        def quantize_h(h):
+            words = hid.tile([P, HALF], U32, name="hwords", align_bytes=64)
+            scales = hid.tile([P, HALF], U8, name="hscales", align_bytes=64)
+            nc.vector.quantize_mx(out=words[:].bitcast(FP8X4), scales=scales[:], in_=h[:].rearrange("p n t -> p (n t)"))
+            return words, scales
+
+        order = [(m, e, k, g) for e in range(E) for g in range(2) for m in "13" for k in range(2)]
+        wmat = {"1": w1, "3": w3}
+        raw_of, plane_of, mid_of, w2raw, w2mid, w2q, hq, ra_of, gate_of, bank_of, y_of = {}, {}, {}, {}, {}, {}, {}, {}, {}, {}, {}
+
+        def issue(i):
+            m, e, k, g = order[i]
+            raw_of[i] = load_w(wmat[m], e, k, g)
+
+        def load_gate(e):
+            tile = keep.tile([P, C], F32, name="gate%d" % e)
+            nc.sync.dma_start(tile[:], gate[:, e * C:(e + 1) * C])
+            gate_of[e] = tile
+
+        g4_of, xi_of = {}, {}
+
+        def gather(g, t):
+            if t == 0:
+                g4_of[g] = toks.tile([P, PACK, SLOTS], F32, name="g4")
+            nc.vector.tensor_copy(g4_of[g][:, t, :], plane_of[g, t][:].indirect(offsets[:]))
+
+        def weave(i):
+            mid_of[i] = interleave_w(raw_of[i], SHARES[i])
+
+        def quant(i):
+            wq[order[i]] = quantize_w(mid_of[i])
+
+        def first_half(e, g):
+            for s in range(2):
+                ra_of[e, g, s] = relu(matmuls("1", e, g, s))
+
+        def second_matmuls(e, g):
+            for s in range(2):
+                bank_of[e, g, s] = matmuls("3", e, g, s)
+
+        def second_half(e, g):
+            hs = [product(bank_of[e, g, s], ra_of[e, g, s]) for s in range(2)]
+            for s in range(2):
+                hq[e, g, s] = quantize_h(hs[s])
+
+        def finish(e):
+            bank = psum_y.tile([P, 2, HALF], F32, name="banky")
+            for s in range(2):
+                for g in range(2):
+                    nc.tensor.matmul_mx(
+                        out=bank[:, s, :],
+                        lhsT=w2q[e][0][:, g * N:(g + 1) * N].bitcast(FP8X4), lhsT_scale=w2q[e][1][:, g * N:(g + 1) * N],
+                        rhs=hq[e, g, s][0][:].bitcast(FP8X4), rhs_scale=hq[e, g, s][1][:],
+                        start=(g == 0), stop=(g == 1))
+            y = hid.tile([P, C], F32, name="y")
+            nc.scalar.copy(y[:], bank[:].rearrange("p s n -> p (s n)"))
+            y_of[e] = y
+
+        def scatter(e):
+            y = y_of[e]
+            nc.vector.tensor_tensor(window[:].indirect(offsets[:, e * 16:(e + 1) * 16]), y[:], gate_of[e][:], MULT)
+
+        def load_planes(g, ts):
+            for t in ts:
+                plane_of[g, t] = load_plane(g, t)
+
+        issue(0)
+        load_planes(0, (0, 1))
+        issue(1)
+        load_planes(0, (2, 3))
+        issue(2)
+        load_planes(1, (0, 1))
+        issue(3)
+        load_planes(1, (2, 3))
+        issue(4)
+        issue(5)
+        issue(6)
+        issue(7)
+        w2raw[0] = load_w2(0)
+        load_gate(0)
+
+        weave(0)
+        gather(0, 0)
+        quant(0)
+        gather(0, 1)
+        weave(1)
+        gather(0, 2)
+        quant(1)
+        gather(0, 3)
+        weave(2)
+        xi = interleave_x(g4_of[0])
+        gather(1, 0)
+        quant(2)
+        gather(1, 1)
+        xq.append(quantize_x(xi))
+        weave(3)
+        gather(1, 2)
+        quant(3)
+        gather(1, 3)
+        xi = interleave_x(g4_of[1])
+        for i in range(4, 16):
+            if i + 4 < 16:
+                issue(i + 4)
+            if i + 4 == 15:
+                w2raw[1] = load_w2(1)
+                load_gate(1)
+            weave(i)
+            if i > 4:
+                quant(i - 1)
+            else:
+                xq.append(quantize_x(xi))
+            if i in (5, 7, 11, 15):
+                e, g = (0, 0) if i == 5 else order[i - 3][1::2]
+                first_half(e, g)
+            if i in (5, 8, 12):
+                e, g = (0, 0) if i == 5 else order[i - 4][1::2]
+                second_matmuls(e, g)
+            if i in (6, 9, 13):
+                e, g = (0, 0) if i == 6 else order[i - 5][1::2]
+                second_half(e, g)
+            if i == 8:
+                w2mid[0] = interleave_w2(0, w2raw[0])
+            if i == 9:
+                w2q[0] = quantize_w2(0, w2mid[0])
+            if i == 10:
+                finish(0)
+            if i == 11:
+                scatter(0)
+        w2mid[1] = interleave_w2(1, w2raw[1])
+        quant(15)
+        w2q[1] = quantize_w2(1, w2mid[1])
+        second_matmuls(1, 1)
+        second_half(1, 1)
+        finish(1)
+        scatter(1)
+        nc.sync.dma_start(out, window[:])

@@ -19,19 +19,20 @@ PACK = 4
 PASS = P * PACK
 SLOTS = E * C
 HALF = 128
-SHARES = [32] * 4 + [56] * 10 + [72, 88]
+PINS = {13: "pin_ra10", 5: "pin_ra00", 12: "pin_y0"}
+SHARES = [88,88,64,64,40,40,128,128,0,0,64,64,56,56,40,96]
 
 
 def tile_routed_moe_kernel(tc, xT, w1, w3, w2, gate, offs, out):
     nc = tc.nc
     with ExitStack() as ctx:
         keep = ctx.enter_context(tc.tile_pool(name="keep", bufs=1))
-        planes = ctx.enter_context(tc.tile_pool(name="planes", bufs=8))
-        raws = ctx.enter_context(tc.tile_pool(name="raws", bufs=8))
-        mids = ctx.enter_context(tc.tile_pool(name="mids", bufs=3))
+        planes = ctx.enter_context(tc.tile_pool(name="planes", bufs=6))
+        raws = ctx.enter_context(tc.tile_pool(name="raws", bufs=7))
+        mids = ctx.enter_context(tc.tile_pool(name="mids", bufs=4))
         codes = ctx.enter_context(tc.tile_pool(name="codes", bufs=16))
         toks = ctx.enter_context(tc.tile_pool(name="toks", bufs=2))
-        hid = ctx.enter_context(tc.tile_pool(name="hid", bufs=4))
+        hid = ctx.enter_context(tc.tile_pool(name="hid", bufs=2))
         psum = ctx.enter_context(tc.psum_pool(name="psum", bufs=3))
         psum_y = ctx.enter_context(tc.psum_pool(name="psum_y", bufs=2))
 
@@ -58,13 +59,17 @@ def tile_routed_moe_kernel(tc, xT, w1, w3, w2, gate, offs, out):
             nc.sync.dma_start(raw[:], w2[e].rearrange("(g p j) n -> p g j n", p=P, j=PACK))
             return raw
 
-        def interleave_w(raw, share):
-            mid = mids.tile([P, PACK * PASS], BF16, name="mid", align_bytes=64)
+        def interleave_w(raw, share, pin):
+            if pin:
+                mid = keep.tile([P, PACK * PASS], BF16, name="mid", tag=pin, align_bytes=64)
+            else:
+                mid = mids.tile([P, PACK * PASS], BF16, name="mid", align_bytes=64)
             dst = mid[:].rearrange("p (t m j) -> p m j t", t=PACK, j=PACK)
             src = raw[:].rearrange("p j (m t) -> p m j t", t=PACK)
             if share:
                 nc.vector.tensor_copy(dst[:, 0:share], src[:, 0:share])
-            nc.scalar.copy(dst[:, share:P], src[:, share:P])
+            if share < P:
+                nc.scalar.copy(dst[:, share:P], src[:, share:P])
             return mid
 
         def quantize_w(mid):
@@ -112,19 +117,9 @@ def tile_routed_moe_kernel(tc, xT, w1, w3, w2, gate, offs, out):
                         start=(k == 0), stop=(k == 1))
             return bank
 
-        def relu(bank):
-            ra = hid.tile([P, HALF, PACK], F32, name="ra")
-            nc.scalar.activation(ra[:], bank[:].rearrange("p t n -> p n t"), RELU)
-            return ra
-
-        def product(bank, ra):
-            h = hid.tile([P, HALF, PACK], BF16, name="h", align_bytes=64)
-            nc.vector.tensor_tensor(h[:], bank[:].rearrange("p t n -> p n t"), ra[:], MULT)
-            return h
-
         def quantize_h(h):
-            words = hid.tile([P, HALF], U32, name="hwords", align_bytes=64)
-            scales = hid.tile([P, HALF], U8, name="hscales", align_bytes=64)
+            words = toks.tile([P, C], U32, name="hwords", align_bytes=64)
+            scales = toks.tile([P, C], U8, name="hscales", align_bytes=64)
             nc.vector.quantize_mx(out=words[:].bitcast(FP8X4), scales=scales[:], in_=h[:].rearrange("p n t -> p (n t)"))
             return words, scales
 
@@ -149,112 +144,78 @@ def tile_routed_moe_kernel(tc, xT, w1, w3, w2, gate, offs, out):
             nc.vector.tensor_copy(g4_of[g][:, t, :], plane_of[g, t][:].indirect(offsets[:]))
 
         def weave(i):
-            mid_of[i] = interleave_w(raw_of[i], SHARES[i])
+            mid_of[i] = interleave_w(raw_of[i], SHARES[i], PINS.get(i))
 
         def quant(i):
             wq[order[i]] = quantize_w(mid_of[i])
 
         def first_half(e, g):
+            tag = "pin_ra%d%d" % (e, g)
+            if tag in PINS.values():
+                ra = keep.tile([P, 2, HALF, PACK], F32, name="ra", tag=tag, align_bytes=64)
+            else:
+                ra = hid.tile([P, 2, HALF, PACK], F32, name="ra")
             for s in range(2):
-                ra_of[e, g, s] = relu(matmuls("1", e, g, s))
-
-        def second_matmuls(e, g):
-            for s in range(2):
-                bank_of[e, g, s] = matmuls("3", e, g, s)
+                bank = matmuls("1", e, g, s)
+                nc.scalar.activation(ra[:, s], bank[:].rearrange("p t n -> p n t"), RELU)
+            ra_of[e, g] = ra
 
         def second_half(e, g):
-            hs = [product(bank_of[e, g, s], ra_of[e, g, s]) for s in range(2)]
+            h = hid.tile([P, C, PACK], BF16, name="h", align_bytes=64)
             for s in range(2):
-                hq[e, g, s] = quantize_h(hs[s])
+                bank = matmuls("3", e, g, s)
+                nc.vector.tensor_tensor(h[:, s * HALF:(s + 1) * HALF, :], bank[:].rearrange("p t n -> p n t"), ra_of[e, g][:, s], MULT)
+            hq[e, g] = quantize_h(h)
 
         def finish(e):
-            bank = psum_y.tile([P, 2, HALF], F32, name="banky")
-            for s in range(2):
-                for g in range(2):
-                    nc.tensor.matmul_mx(
-                        out=bank[:, s, :],
-                        lhsT=w2q[e][0][:, g * N:(g + 1) * N].bitcast(FP8X4), lhsT_scale=w2q[e][1][:, g * N:(g + 1) * N],
-                        rhs=hq[e, g, s][0][:].bitcast(FP8X4), rhs_scale=hq[e, g, s][1][:],
-                        start=(g == 0), stop=(g == 1))
-            y = hid.tile([P, C], F32, name="y")
-            nc.scalar.copy(y[:], bank[:].rearrange("p s n -> p (s n)"))
-            y_of[e] = y
-
-        def scatter(e):
-            y = y_of[e]
+            bank = psum_y.tile([P, C], F32, name="banky")
+            for g in range(2):
+                nc.tensor.matmul_mx(
+                    out=bank[:],
+                    lhsT=w2q[e][0][:, g * N:(g + 1) * N].bitcast(FP8X4), lhsT_scale=w2q[e][1][:, g * N:(g + 1) * N],
+                    rhs=hq[e, g][0][:].bitcast(FP8X4), rhs_scale=hq[e, g][1][:],
+                    start=(g == 0), stop=(g == 1))
+            if "pin_y%d" % e in PINS.values():
+                y = keep.tile([P, C], F32, name="y", tag="pin_y%d" % e, align_bytes=64)
+            else:
+                y = hid.tile([P, C], F32, name="y")
+            nc.scalar.copy(y[:], bank[:])
             nc.vector.tensor_tensor(window[:].indirect(offsets[:, e * 16:(e + 1) * 16]), y[:], gate_of[e][:], MULT)
 
         def load_planes(g, ts):
             for t in ts:
                 plane_of[g, t] = load_plane(g, t)
 
-        issue(0)
-        load_planes(0, (0, 1))
-        issue(1)
-        load_planes(0, (2, 3))
-        issue(2)
-        load_planes(1, (0, 1))
-        issue(3)
-        load_planes(1, (2, 3))
-        issue(4)
-        issue(5)
-        issue(6)
-        issue(7)
-        w2raw[0] = load_w2(0)
-        load_gate(0)
-
-        weave(0)
-        gather(0, 0)
-        quant(0)
-        gather(0, 1)
-        weave(1)
-        gather(0, 2)
-        quant(1)
-        gather(0, 3)
-        weave(2)
-        xi = interleave_x(g4_of[0])
-        gather(1, 0)
-        quant(2)
-        gather(1, 1)
-        xq.append(quantize_x(xi))
-        weave(3)
-        gather(1, 2)
-        quant(3)
-        gather(1, 3)
-        xi = interleave_x(g4_of[1])
-        for i in range(4, 16):
+        STEPS = ((0, 0, 5, 5), (0, 1, 5, 7), (1, 0, 13, 13), (1, 1, 13, 15))
+        Y0 = 12
+        for g in range(2):
+            load_planes(g, range(PACK))
+            for t in range(PACK):
+                gather(g, t)
+            xq.append(quantize_x(interleave_x(g4_of[g])))
+        for i in range(4):
+            issue(i)
+        for i in range(16):
             if i + 4 < 16:
                 issue(i + 4)
+            if i + 4 == 7:
+                w2raw[0] = load_w2(0)
+                load_gate(0)
             if i + 4 == 15:
                 w2raw[1] = load_w2(1)
                 load_gate(1)
             weave(i)
-            if i > 4:
-                quant(i - 1)
-            else:
-                xq.append(quantize_x(xi))
-            if i in (5, 7, 11, 15):
-                e, g = (0, 0) if i == 5 else order[i - 3][1::2]
-                first_half(e, g)
-            if i in (5, 8, 12):
-                e, g = (0, 0) if i == 5 else order[i - 4][1::2]
-                second_matmuls(e, g)
-            if i in (6, 9, 13):
-                e, g = (0, 0) if i == 6 else order[i - 5][1::2]
-                second_half(e, g)
             if i == 8:
-                w2mid[0] = interleave_w2(0, w2raw[0])
-            if i == 9:
-                w2q[0] = quantize_w2(0, w2mid[0])
-            if i == 10:
+                w2q[0] = quantize_w2(0, interleave_w2(0, w2raw[0]))
+            if i == 15:
+                w2q[1] = quantize_w2(1, interleave_w2(1, w2raw[1]))
+            quant(i)
+            for e, g, first, second in STEPS:
+                if i == first:
+                    first_half(e, g)
+                if i == second:
+                    second_half(e, g)
+            if i == Y0:
                 finish(0)
-            if i == 11:
-                scatter(0)
-        w2mid[1] = interleave_w2(1, w2raw[1])
-        quant(15)
-        w2q[1] = quantize_w2(1, w2mid[1])
-        second_matmuls(1, 1)
-        second_half(1, 1)
         finish(1)
-        scatter(1)
         nc.sync.dma_start(out, window[:])

@@ -64,8 +64,8 @@ def tile_routed_moe_kernel(tc, xT, w1, w3, w2, gate, offs, out):
                 mid = keep.tile([P, PACK * PASS], BF16, name="mid", tag=pin, align_bytes=64)
             else:
                 mid = mids.tile([P, PACK * PASS], BF16, name="mid", align_bytes=64)
-            dst = mid[:].rearrange("p (t m j) -> p m j t", t=PACK, j=PACK)
-            src = raw[:].rearrange("p j (m t) -> p m j t", t=PACK)
+            dst = mid[:].rearrange("p (t m j) -> p m t j", t=PACK, j=PACK)
+            src = raw[:].rearrange("p j (m t) -> p m t j", t=PACK)
             if share:
                 nc.vector.tensor_copy(dst[:, 0:share], src[:, 0:share])
             if share < P:

@@ -19,138 +19,117 @@ PACK = 4
 PASS = P * PACK
 SLOTS = E * C
 HALF = 128
-PINS = {13: "pin_ra10", 5: "pin_ra00", 12: "pin_y0"}
-SHARES = [88,88,64,64,40,40,128,128,0,0,64,64,56,56,40,96]
+SHARES = [0,128,128,0,128,128,128,0,88,0,88,0,72,0,128,56]
+PINS = {3: "ra01", 7: "ra10"}
 
 
 def tile_routed_moe_kernel(tc, xT, w1, w3, w2, gate, offs, out):
     nc = tc.nc
     with ExitStack() as ctx:
         keep = ctx.enter_context(tc.tile_pool(name="keep", bufs=1))
-        planes = ctx.enter_context(tc.tile_pool(name="planes", bufs=6))
-        raws = ctx.enter_context(tc.tile_pool(name="raws", bufs=7))
+        raws = ctx.enter_context(tc.tile_pool(name="raws", bufs=5))
         mids = ctx.enter_context(tc.tile_pool(name="mids", bufs=4))
-        codes = ctx.enter_context(tc.tile_pool(name="codes", bufs=16))
         toks = ctx.enter_context(tc.tile_pool(name="toks", bufs=2))
         hid = ctx.enter_context(tc.tile_pool(name="hid", bufs=2))
-        psum = ctx.enter_context(tc.psum_pool(name="psum", bufs=3))
-        psum_y = ctx.enter_context(tc.psum_pool(name="psum_y", bufs=2))
+        psum = {"1": ctx.enter_context(tc.psum_pool(name="psum_a", bufs=4)), "3": ctx.enter_context(tc.psum_pool(name="psum_b", bufs=3))}
+        psum_y = ctx.enter_context(tc.psum_pool(name="psum_y", bufs=1))
 
         offsets = keep.tile([P, SLOTS // 16], U16, name="offsets")
         nc.sync.dma_start(offsets[:], offs)
         window = keep.tile([P, T], F32, name="window")
         nc.vector.memset(window[:], 0.0)
 
+        def quantize(pool, key, mid, width):
+            words = pool.tile([P, width], U32, name="words" + key, align_bytes=64)
+            scales = pool.tile([P, width], U8, name="scales" + key, align_bytes=64)
+            nc.vector.quantize_mx(out=words[:].bitcast(FP8X4), scales=scales[:], in_=mid)
+            return words, scales
+
         xTv = xT.rearrange("(g p t) n -> g p t n", p=P, t=PACK)
+        xq = []
+        raw_x = {}
 
-        def load_w(w, e, k, g):
-            raw = raws.tile([P, PACK, PASS], F32, name="raw")
-            src = w[e, k * PASS:(k + 1) * PASS, g * PASS:(g + 1) * PASS]
+        def load_x(g, u):
+            raw = raws.tile([P, 2, T], F32, name="raw")
+            nc.sync.dma_start(raw[:], xTv[g, :, 2 * u:2 * u + 2, :])
+            raw_x[g, u] = raw
+
+        def gather(g):
+            g4 = toks.tile([P, PACK, SLOTS], F32, name="g4")
+            for t in range(PACK):
+                nc.vector.tensor_copy(g4[:, t, :], raw_x[g, t // 2][:, t % 2, :].indirect(offsets[:]))
+            xi = toks.tile([P, SLOTS, PACK], BF16, name="xi", align_bytes=64)
+            nc.scalar.copy(xi[:], g4[:].rearrange("p t n -> p n t"))
+            xq.append(quantize(toks, "x", xi[:].rearrange("p n t -> p (n t)"), SLOTS))
+
+        pieces = [(m, e, k, (0, 1)) for e in range(E) for m in "13" for k in range(2)]
+        pieces[7:] = [("3", 1, 1, (0,)), ("3", 1, 1, (1,))]
+        wmat = {"1": w1, "3": w3}
+        raw_w, mid_w, wq = {}, {}, {}
+
+        def load_w(i):
+            m, e, k, gs = pieces[i]
+            raw = raws.tile([P, PACK, len(gs) * PASS], F32, name="raw")
+            src = wmat[m][e, k * PASS:(k + 1) * PASS, gs[0] * PASS:(gs[-1] + 1) * PASS]
             nc.sync.dma_start(raw[:], src.rearrange("(p j) c -> p j c", j=PACK))
-            return raw
+            raw_w[i] = raw
 
-        def load_plane(g, t):
-            plane = planes.tile([P, T], F32, name="plane")
-            nc.sync.dma_start(plane[:], xTv[g, :, t, :])
-            return plane
+        def weave(i):
+            m, e, k, gs = pieces[i]
+            shape = [P, len(gs), PACK * PASS]
+            if i in PINS:
+                mid = keep.tile(shape, BF16, name="mid", tag=PINS[i], align_bytes=64)
+            else:
+                mid = mids.tile(shape, BF16, name="mid", align_bytes=64)
+            for n, g in enumerate(gs):
+                src = raw_w[i][:, :, n * PASS:(n + 1) * PASS].rearrange("p j (m t) -> p m t j", t=PACK)
+                dst = mid[:, n].rearrange("p (t m j) -> p m t j", t=PACK, j=PACK)
+                share = SHARES[2 * i + n] if i < 7 else SHARES[7 + i]
+                if share > 0:
+                    nc.vector.tensor_copy(dst[:, :share], src[:, :share])
+                if share < P:
+                    nc.scalar.copy(dst[:, share:], src[:, share:])
+            mid_w[i] = mid
 
-        def load_w2(e):
+        def quant(i):
+            m, e, k, gs = pieces[i]
+            words, scales = quantize(keep, "w%d" % i, mid_w[i][:].rearrange("p g c -> p (g c)"), len(gs) * PASS)
+            for n, g in enumerate(gs):
+                wq[m, e, k, g] = words, scales, n * PASS
+
+        w2q, raw_w2, gate_of = {}, {}, {}
+
+        def load_tail(e):
             raw = keep.tile([P, 2, PACK, N], F32, name="w2raw%d" % e)
             nc.sync.dma_start(raw[:], w2[e].rearrange("(g p j) n -> p g j n", p=P, j=PACK))
-            return raw
-
-        def interleave_w(raw, share, pin):
-            if pin:
-                mid = keep.tile([P, PACK * PASS], BF16, name="mid", tag=pin, align_bytes=64)
-            else:
-                mid = mids.tile([P, PACK * PASS], BF16, name="mid", align_bytes=64)
-            dst = mid[:].rearrange("p (t m j) -> p m t j", t=PACK, j=PACK)
-            src = raw[:].rearrange("p j (m t) -> p m t j", t=PACK)
-            if share:
-                nc.vector.tensor_copy(dst[:, 0:share], src[:, 0:share])
-            if share < P:
-                nc.scalar.copy(dst[:, share:P], src[:, share:P])
-            return mid
-
-        def quantize_w(mid):
-            words = codes.tile([P, PASS], U32, name="words", align_bytes=64)
-            scales = codes.tile([P, PASS], U8, name="scales", align_bytes=64)
-            nc.vector.quantize_mx(out=words[:].bitcast(FP8X4), scales=scales[:], in_=mid[:])
-            return words, scales
-
-        def interleave_x(g4):
-            xi = toks.tile([P, SLOTS, PACK], BF16, name="xi", align_bytes=64)
-            nc.scalar.copy(xi[:].rearrange("p (c i) t -> p c t i", i=4), g4[:].rearrange("p t (c i) -> p c t i", i=4))
-            return xi
-
-        def quantize_x(xi):
-            words = toks.tile([P, SLOTS], U32, name="xwords", align_bytes=64)
-            scales = toks.tile([P, SLOTS], U8, name="xscales", align_bytes=64)
-            nc.vector.quantize_mx(out=words[:].bitcast(FP8X4), scales=scales[:], in_=xi[:].rearrange("p n t -> p (n t)"))
-            return words, scales
-
-        def interleave_w2(e, raw):
-            mid = keep.tile([P, 2, N, PACK], BF16, name="w2mid%d" % e, align_bytes=64)
-            for g, copy in ((0, nc.vector.tensor_copy), (1, nc.scalar.copy)):
-                copy(mid[:, g].rearrange("p (c i) j -> p c j i", i=4), raw[:, g].rearrange("p j (c i) -> p c j i", i=4))
-            return mid
-
-        def quantize_w2(e, mid):
-            words = keep.tile([P, 2 * N], U32, name="w2words%d" % e, align_bytes=64)
-            scales = keep.tile([P, 2 * N], U8, name="w2scales%d" % e, align_bytes=64)
-            nc.vector.quantize_mx(out=words[:].bitcast(FP8X4), scales=scales[:], in_=mid[:].rearrange("p g n j -> p (g n j)"))
-            return words, scales
-
-        xq = []
-        wq = {}
-
-        def matmuls(mat, e, g, s):
-            bank = psum.tile([P, PACK, HALF], F32, name="bank" + mat)
-            cols = slice(e * C + s * HALF, e * C + (s + 1) * HALF)
-            for t in range(PACK):
-                for k in range(2):
-                    words, scales = wq[mat, e, k, g]
-                    nc.tensor.matmul_mx(
-                        out=bank[:, t, :],
-                        lhsT=words[:, t * P:(t + 1) * P].bitcast(FP8X4), lhsT_scale=scales[:, t * P:(t + 1) * P],
-                        rhs=xq[k][0][:, cols].bitcast(FP8X4), rhs_scale=xq[k][1][:, cols],
-                        start=(k == 0), stop=(k == 1))
-            return bank
-
-        def quantize_h(h):
-            words = toks.tile([P, C], U32, name="hwords", align_bytes=64)
-            scales = toks.tile([P, C], U8, name="hscales", align_bytes=64)
-            nc.vector.quantize_mx(out=words[:].bitcast(FP8X4), scales=scales[:], in_=h[:].rearrange("p n t -> p (n t)"))
-            return words, scales
-
-        order = [(m, e, k, g) for e in range(E) for g in range(2) for m in "13" for k in range(2)]
-        wmat = {"1": w1, "3": w3}
-        raw_of, plane_of, mid_of, w2raw, w2mid, w2q, hq, ra_of, gate_of, bank_of, y_of = {}, {}, {}, {}, {}, {}, {}, {}, {}, {}, {}
-
-        def issue(i):
-            m, e, k, g = order[i]
-            raw_of[i] = load_w(wmat[m], e, k, g)
-
-        def load_gate(e):
+            raw_w2[e] = raw
             tile = keep.tile([P, C], F32, name="gate%d" % e)
             nc.sync.dma_start(tile[:], gate[:, e * C:(e + 1) * C])
             gate_of[e] = tile
 
-        g4_of, xi_of = {}, {}
+        def quant_w2(e):
+            mid = keep.tile([P, 2, N, PACK], BF16, name="w2mid%d" % e, align_bytes=64)
+            nc.scalar.copy(mid[:], raw_w2[e][:].rearrange("p g j n -> p g n j"))
+            w2q[e] = quantize(keep, "v%d" % e, mid[:].rearrange("p g n j -> p (g n j)"), 2 * N)
 
-        def gather(g, t):
-            if t == 0:
-                g4_of[g] = toks.tile([P, PACK, SLOTS], F32, name="g4")
-            nc.vector.tensor_copy(g4_of[g][:, t, :], plane_of[g, t][:].indirect(offsets[:]))
+        hq, ra_of = {}, {}
 
-        def weave(i):
-            mid_of[i] = interleave_w(raw_of[i], SHARES[i], PINS.get(i))
-
-        def quant(i):
-            wq[order[i]] = quantize_w(mid_of[i])
+        def matmuls(m, e, g, s):
+            bank = psum[m].tile([P, PACK, HALF], F32, name="bank" + m)
+            cols = slice(e * C + s * HALF, e * C + (s + 1) * HALF)
+            for t in range(PACK):
+                for k in range(2):
+                    words, scales, at = wq[m, e, k, g]
+                    feats = slice(at + t * P, at + (t + 1) * P)
+                    nc.tensor.matmul_mx(
+                        out=bank[:, t, :],
+                        lhsT=words[:, feats].bitcast(FP8X4), lhsT_scale=scales[:, feats],
+                        rhs=xq[k][0][:, cols].bitcast(FP8X4), rhs_scale=xq[k][1][:, cols],
+                        start=(k == 0), stop=(k == 1))
+            return bank
 
         def first_half(e, g):
-            tag = "pin_ra%d%d" % (e, g)
+            tag = "ra%d%d" % (e, g)
             if tag in PINS.values():
                 ra = keep.tile([P, 2, HALF, PACK], F32, name="ra", tag=tag, align_bytes=64)
             else:
@@ -165,57 +144,48 @@ def tile_routed_moe_kernel(tc, xT, w1, w3, w2, gate, offs, out):
             for s in range(2):
                 bank = matmuls("3", e, g, s)
                 nc.vector.tensor_tensor(h[:, s * HALF:(s + 1) * HALF, :], bank[:].rearrange("p t n -> p n t"), ra_of[e, g][:, s], MULT)
-            hq[e, g] = quantize_h(h)
+            hq[e, g] = quantize(hid, "h", h[:].rearrange("p n t -> p (n t)"), C)
 
         def finish(e):
             bank = psum_y.tile([P, C], F32, name="banky")
+            words, scales = w2q[e]
             for g in range(2):
+                cols = slice(g * N, (g + 1) * N)
                 nc.tensor.matmul_mx(
                     out=bank[:],
-                    lhsT=w2q[e][0][:, g * N:(g + 1) * N].bitcast(FP8X4), lhsT_scale=w2q[e][1][:, g * N:(g + 1) * N],
+                    lhsT=words[:, cols].bitcast(FP8X4), lhsT_scale=scales[:, cols],
                     rhs=hq[e, g][0][:].bitcast(FP8X4), rhs_scale=hq[e, g][1][:],
                     start=(g == 0), stop=(g == 1))
-            if "pin_y%d" % e in PINS.values():
-                y = keep.tile([P, C], F32, name="y", tag="pin_y%d" % e, align_bytes=64)
-            else:
-                y = hid.tile([P, C], F32, name="y")
+            y = hid.tile([P, C], F32, name="y")
             nc.scalar.copy(y[:], bank[:])
             nc.vector.tensor_tensor(window[:].indirect(offsets[:, e * 16:(e + 1) * 16]), y[:], gate_of[e][:], MULT)
 
-        def load_planes(g, ts):
-            for t in ts:
-                plane_of[g, t] = load_plane(g, t)
-
-        STEPS = ((0, 0, 5, 5), (0, 1, 5, 7), (1, 0, 13, 13), (1, 1, 13, 15))
-        Y0 = 12
         for g in range(2):
-            load_planes(g, range(PACK))
-            for t in range(PACK):
-                gather(g, t)
-            xq.append(quantize_x(interleave_x(g4_of[g])))
-        for i in range(4):
-            issue(i)
-        for i in range(16):
-            if i + 4 < 16:
-                issue(i + 4)
-            if i + 4 == 7:
-                w2raw[0] = load_w2(0)
-                load_gate(0)
-            if i + 4 == 15:
-                w2raw[1] = load_w2(1)
-                load_gate(1)
+            for u in range(2):
+                load_x(g, u)
+            gather(g)
+        for i in range(3):
+            load_w(i)
+        for i in range(9):
+            if i + 3 < 9:
+                load_w(i + 3)
+            if i == 0:
+                load_tail(0)
+            if i == 5:
+                load_tail(1)
             weave(i)
-            if i == 8:
-                w2q[0] = quantize_w2(0, interleave_w2(0, w2raw[0]))
-            if i == 15:
-                w2q[1] = quantize_w2(1, interleave_w2(1, w2raw[1]))
             quant(i)
-            for e, g, first, second in STEPS:
-                if i == first:
-                    first_half(e, g)
-                if i == second:
-                    second_half(e, g)
-            if i == Y0:
+            if i == 3:
+                quant_w2(0)
+                for g in range(2):
+                    first_half(0, g)
+                    second_half(0, g)
                 finish(0)
+            if i == 7:
+                first_half(1, 0)
+                second_half(1, 0)
+                first_half(1, 1)
+        quant_w2(1)
+        second_half(1, 1)
         finish(1)
         nc.sync.dma_start(out, window[:])

from contextlib import ExitStack

import concourse.mybir as mybir

K, T, E, C, H, N = 1024, 1536, 2, 256, 1024, 128
FLOPS = 2 * E * C * (2 * K * H + H * N)

F32 = mybir.dt.float32
BF16 = mybir.dt.bfloat16
U32 = mybir.dt.uint32
U16 = mybir.dt.uint16
U8 = mybir.dt.uint8
FP8X4 = mybir.dt.float8_e4m3fn_x4
MULT = mybir.AluOpType.mult
RELU = mybir.ActivationFunctionType.Relu

P = 128
PACK = 4
PASS = P * PACK
SLOTS = E * C
HALF = 128
SHARES = [0,128,128,0,128,128,128,0,88,0,88,0,72,0,128,56]
PINS = {3: "ra01", 7: "ra10"}


def tile_routed_moe_kernel(tc, xT, w1, w3, w2, gate, offs, out):
    nc = tc.nc
    with ExitStack() as ctx:
        keep = ctx.enter_context(tc.tile_pool(name="keep", bufs=1))
        raws = ctx.enter_context(tc.tile_pool(name="raws", bufs=5))
        mids = ctx.enter_context(tc.tile_pool(name="mids", bufs=4))
        toks = ctx.enter_context(tc.tile_pool(name="toks", bufs=2))
        hid = ctx.enter_context(tc.tile_pool(name="hid", bufs=2))
        psum = {"1": ctx.enter_context(tc.psum_pool(name="psum_a", bufs=4)), "3": ctx.enter_context(tc.psum_pool(name="psum_b", bufs=3))}
        psum_y = ctx.enter_context(tc.psum_pool(name="psum_y", bufs=1))

        offsets = keep.tile([P, SLOTS // 16], U16, name="offsets")
        nc.sync.dma_start(offsets[:], offs)
        window = keep.tile([P, T], F32, name="window")
        nc.vector.memset(window[:], 0.0)

        def quantize(pool, key, mid, width):
            words = pool.tile([P, width], U32, name="words" + key, align_bytes=64)
            scales = pool.tile([P, width], U8, name="scales" + key, align_bytes=64)
            nc.vector.quantize_mx(out=words[:].bitcast(FP8X4), scales=scales[:], in_=mid)
            return words, scales

        xTv = xT.rearrange("(g p t) n -> g p t n", p=P, t=PACK)
        xq = []
        raw_x = {}

        def load_x(g, u):
            raw = raws.tile([P, 2, T], F32, name="raw")
            nc.sync.dma_start(raw[:], xTv[g, :, 2 * u:2 * u + 2, :])
            raw_x[g, u] = raw

        def gather(g):
            g4 = toks.tile([P, PACK, SLOTS], F32, name="g4")
            for t in range(PACK):
                nc.vector.tensor_copy(g4[:, t, :], raw_x[g, t // 2][:, t % 2, :].indirect(offsets[:]))
            xi = toks.tile([P, SLOTS, PACK], BF16, name="xi", align_bytes=64)
            nc.scalar.copy(xi[:], g4[:].rearrange("p t n -> p n t"))
            xq.append(quantize(toks, "x", xi[:].rearrange("p n t -> p (n t)"), SLOTS))

        pieces = [(m, e, k, (0, 1)) for e in range(E) for m in "13" for k in range(2)]
        pieces[7:] = [("3", 1, 1, (0,)), ("3", 1, 1, (1,))]
        wmat = {"1": w1, "3": w3}
        raw_w, mid_w, wq = {}, {}, {}

        def load_w(i):
            m, e, k, gs = pieces[i]
            raw = raws.tile([P, PACK, len(gs) * PASS], F32, name="raw")
            src = wmat[m][e, k * PASS:(k + 1) * PASS, gs[0] * PASS:(gs[-1] + 1) * PASS]
            nc.sync.dma_start(raw[:], src.rearrange("(p j) c -> p j c", j=PACK))
            raw_w[i] = raw

        def weave(i):
            m, e, k, gs = pieces[i]
            shape = [P, len(gs), PACK * PASS]
            if i in PINS:
                mid = keep.tile(shape, BF16, name="mid", tag=PINS[i], align_bytes=64)
            else:
                mid = mids.tile(shape, BF16, name="mid", align_bytes=64)
            for n, g in enumerate(gs):
                src = raw_w[i][:, :, n * PASS:(n + 1) * PASS].rearrange("p j (m t) -> p m t j", t=PACK)
                dst = mid[:, n].rearrange("p (t m j) -> p m t j", t=PACK, j=PACK)
                share = SHARES[2 * i + n] if i < 7 else SHARES[7 + i]
                if share > 0:
                    nc.vector.tensor_copy(dst[:, :share], src[:, :share])
                if share < P:
                    nc.scalar.copy(dst[:, share:], src[:, share:])
            mid_w[i] = mid

        def quant(i):
            m, e, k, gs = pieces[i]
            words, scales = quantize(keep, "w%d" % i, mid_w[i][:].rearrange("p g c -> p (g c)"), len(gs) * PASS)
            for n, g in enumerate(gs):
                wq[m, e, k, g] = words, scales, n * PASS

        w2q, raw_w2, gate_of = {}, {}, {}

        def load_tail(e):
            raw = keep.tile([P, 2, PACK, N], F32, name="w2raw%d" % e)
            nc.sync.dma_start(raw[:], w2[e].rearrange("(g p j) n -> p g j n", p=P, j=PACK))
            raw_w2[e] = raw
            tile = keep.tile([P, C], F32, name="gate%d" % e)
            nc.sync.dma_start(tile[:], gate[:, e * C:(e + 1) * C])
            gate_of[e] = tile

        def quant_w2(e):
            mid = keep.tile([P, 2, N, PACK], BF16, name="w2mid%d" % e, align_bytes=64)
            nc.scalar.copy(mid[:], raw_w2[e][:].rearrange("p g j n -> p g n j"))
            w2q[e] = quantize(keep, "v%d" % e, mid[:].rearrange("p g n j -> p (g n j)"), 2 * N)

        hq, ra_of = {}, {}

        def matmuls(m, e, g, s):
            bank = psum[m].tile([P, PACK, HALF], F32, name="bank" + m)
            cols = slice(e * C + s * HALF, e * C + (s + 1) * HALF)
            for t in range(PACK):
                for k in range(2):
                    words, scales, at = wq[m, e, k, g]
                    feats = slice(at + t * P, at + (t + 1) * P)
                    nc.tensor.matmul_mx(
                        out=bank[:, t, :],
                        lhsT=words[:, feats].bitcast(FP8X4), lhsT_scale=scales[:, feats],
                        rhs=xq[k][0][:, cols].bitcast(FP8X4), rhs_scale=xq[k][1][:, cols],
                        start=(k == 0), stop=(k == 1))
            return bank

        def first_half(e, g):
            tag = "ra%d%d" % (e, g)
            if tag in PINS.values():
                ra = keep.tile([P, 2, HALF, PACK], F32, name="ra", tag=tag, align_bytes=64)
            else:
                ra = hid.tile([P, 2, HALF, PACK], F32, name="ra")
            for s in range(2):
                bank = matmuls("1", e, g, s)
                nc.scalar.activation(ra[:, s], bank[:].rearrange("p t n -> p n t"), RELU)
            ra_of[e, g] = ra

        def second_half(e, g):
            h = hid.tile([P, C, PACK], BF16, name="h", align_bytes=64)
            for s in range(2):
                bank = matmuls("3", e, g, s)
                nc.vector.tensor_tensor(h[:, s * HALF:(s + 1) * HALF, :], bank[:].rearrange("p t n -> p n t"), ra_of[e, g][:, s], MULT)
            hq[e, g] = quantize(hid, "h", h[:].rearrange("p n t -> p (n t)"), C)

        def finish(e):
            bank = psum_y.tile([P, C], F32, name="banky")
            words, scales = w2q[e]
            for g in range(2):
                cols = slice(g * N, (g + 1) * N)
                nc.tensor.matmul_mx(
                    out=bank[:],
                    lhsT=words[:, cols].bitcast(FP8X4), lhsT_scale=scales[:, cols],
                    rhs=hq[e, g][0][:].bitcast(FP8X4), rhs_scale=hq[e, g][1][:],
                    start=(g == 0), stop=(g == 1))
            y = hid.tile([P, C], F32, name="y")
            nc.scalar.copy(y[:], bank[:])
            nc.vector.tensor_tensor(window[:].indirect(offsets[:, e * 16:(e + 1) * 16]), y[:], gate_of[e][:], MULT)

        for g in range(2):
            for u in range(2):
                load_x(g, u)
            gather(g)
        for i in range(3):
            load_w(i)
        for i in range(9):
            if i + 3 < 9:
                load_w(i + 3)
            if i == 0:
                load_tail(0)
            if i == 5:
                load_tail(1)
            weave(i)
            quant(i)
            if i == 3:
                quant_w2(0)
                for g in range(2):
                    first_half(0, g)
                    second_half(0, g)
                finish(0)
            if i == 7:
                first_half(1, 0)
                second_half(1, 0)
                first_half(1, 1)
        quant_w2(1)
        second_half(1, 1)
        finish(1)
        nc.sync.dma_start(out, window[:])
